import numpy as np
import ml_dtypes


def mxq(x, axis, fmt="e4m3"):
    dtype, down = {"e4m3": (ml_dtypes.float8_e4m3fn, 7), "e5m2": (ml_dtypes.float8_e5m2, 14)}[fmt]
    v = np.moveaxis(np.asarray(x, np.float32).astype(ml_dtypes.bfloat16).astype(np.float64), axis, -1)
    blocks = v.reshape(v.shape[:-1] + (-1, 32))
    amax = np.abs(blocks).max(-1, keepdims=True)
    byte = np.maximum(np.where(amax > 0, np.frexp(amax)[1] - 1 + 127, 0) - down, 1)
    scale = np.exp2(byte - 127.0)
    codes = (blocks / scale).astype(np.float32).astype(dtype).astype(np.float64)
    return np.moveaxis((codes * scale).reshape(v.shape), -1, axis)


WIDE = False


def mx_kscale(k):
    if not WIDE:
        return np.ones(k)
    levels = np.array([10, -10, 5, -5, 0])
    if k % 512:
        return np.exp2(np.random.permutation(np.resize(levels, k // 32))).repeat(32)
    a = np.empty((k // 512, 16))
    for p in range(k // 512):
        a[p, :8] = np.random.permutation(np.resize(levels, 8))
        for g in range(8):
            far = levels[np.abs(levels - a[p, g]) >= 10]
            a[p, g + 8] = far[np.random.randint(len(far))]
    return np.exp2(a.ravel()).repeat(32)


def f64(x):
    return np.asarray(x).astype(np.float64)


def striped(idx):
    return np.tile(idx.reshape(-1, 16).T, (8, 1)).astype(np.uint16)


def unstriped(offs):
    return offs[:16].T.reshape(-1).astype(np.int64)


def pack_weight(w):
    k, n = w.shape
    w = f64(np.asarray(w, np.float32).astype(ml_dtypes.bfloat16)).reshape(k // 32, 32, n)
    amax = np.abs(w).max(1)
    byte = np.clip(np.where(amax > 0, np.frexp(amax)[1] - 1 + 127 - 7, 1), 1, 254)
    scaled = (w * np.exp2(127.0 - byte)[:, None, :]).reshape(k, n).astype(np.float32)
    words = np.ascontiguousarray(scaled.reshape(k // 512, 128, 4, n).transpose(0, 1, 3, 2)).astype(ml_dtypes.float8_e4m3fn).view(np.uint8)
    return words, np.ascontiguousarray(byte.astype(np.uint8).reshape(k // 512, 16, n))


def unpack_weight(words, scales):
    g, p, n, _ = words.shape
    vals = np.ascontiguousarray(words).view(ml_dtypes.float8_e4m3fn).astype(np.float64) * np.repeat(np.exp2(scales.astype(np.float64) - 127.0), 8, axis=1)[..., None]
    return vals.transpose(0, 1, 3, 2).reshape(g * 512, n)


K, T, S, N, H = 1024, 2048, 512, 128, 512


def setup_inputs():
    n = np.random.standard_normal
    s = mx_kscale(K)[:, None]
    u = mx_kscale(H)
    packed_xT = pack_weight(n((K, T)) * s)
    return {
        "x_words": packed_xT[0],
        "x_scales": packed_xT[1],
        "w1": (n((K, H)) / np.sqrt(K) / s).astype(np.float32),
        "w2": (n((K, H)) / np.sqrt(K) / s).astype(np.float32),
        "w3": (n((K, H)) / np.sqrt(K) / s).astype(np.float32),
        "lam": (np.random.uniform(0.3, 0.9, (H, 1))).astype(np.float32),
        "unit": (np.random.uniform(0.6, 1.4, (H, 1)) * u[:, None]).astype(np.float32),
        "w4": (n((H, N)) / np.sqrt(H) / u[:, None]).astype(np.float32),
        "offs": striped(np.random.permutation(T)[:S]),
        "oth": striped(np.random.permutation(S)),
    }


def reference(x_words, x_scales, w1, w2, w3, lam, unit, w4, offs, oth):
    xq = unpack_weight(x_words, x_scales)[:, unstriped(offs)]
    rg = mxq(f64(w2), 0, "e4m3").T @ xq
    eg = np.exp(2.4 * np.tanh(rg))
    egm = eg.mean(axis=1, keepdims=True)
    gt = (np.exp(2.4 * np.tanh(rg))) / (egm + 0.2)
    ro = mxq(f64(w1), 0, "e4m3").T @ xq
    rv = mxq(f64(w3), 0, "e4m3").T @ xq
    adj = ro - (f64(lam) * rv)
    sco = gt * adj
    hid = f64(unit) * (sco - sco[:, unstriped(oth)])
    return mxq(f64(w4), 0, "e4m3").T @ mxq(hid, 0, "e4m3")

@@ -1,0 +1,250 @@
+from contextlib import ExitStack
+
+import concourse.mybir as mybir
+
+K, T, S, N, H = 1024, 2048, 512, 128, 512
+FLOPS = 2 * (3 * K * H * S + H * N * S)
+
+F32 = mybir.dt.float32
+BF16 = mybir.dt.bfloat16
+I32 = mybir.dt.int32
+U32 = mybir.dt.uint32
+U16 = mybir.dt.uint16
+U8 = mybir.dt.uint8
+FP8X4 = mybir.dt.float8_e4m3fn_x4
+ALU = mybir.AluOpType
+ACT = mybir.ActivationFunctionType
+
+P = 128
+PACK = 4
+K_PASS = P * PACK
+PASSES = K // K_PASS
+TILES = H // P
+HALF = S // 2
+PIECE = 128
+PIECES = S // PIECE
+LIST_ROWS = 16
+
+
+def tile_picked_yarmor_pair_p_kernel(
+    tc, x_words, x_scales, w1, w2, w3, lam, unit, w4, offs, oth, out
+):
+    nc = tc.nc
+    with ExitStack() as ctx:
+        keep = ctx.enter_context(tc.tile_pool(name="keep", bufs=1))
+        psum = ctx.enter_context(tc.psum_pool(name="psum", bufs=1))
+
+        def bank(b, width=S):
+            return psum.tile([P, width], F32, name=f"bank{b}", tag=f"bank{b}")
+
+        offs_t = keep.tile([P, S // LIST_ROWS], U16, name="offs_t")
+        oth_t = keep.tile([P, S // LIST_ROWS], U16, name="oth_t")
+        scale_table = keep.tile([P, T], U8, name="scale_table", align_bytes=64)
+        word_table = [keep.tile([P, T], I32, name=f"word_table{g}", align_bytes=64) for g in range(PASSES)]
+        raw = {}
+
+        def load_weight(name, w, g):
+            raw[name, g] = keep.tile([P, PACK, H], F32, name=f"raw_{name}{g}", align_bytes=64)
+            rows = w[g * K_PASS : (g + 1) * K_PASS, :]
+            nc.sync.dma_start(out=raw[name, g][:], in_=rows.rearrange("(p j) c -> p j c", j=PACK))
+
+        def load_scales(g):
+            for q in range(4):
+                first = 32 * q + 4 * g
+                nc.sync.dma_start(
+                    out=scale_table[first : first + 4, :].bitcast(I32),
+                    in_=x_scales[g, 4 * q : 4 * q + 4, :].bitcast(I32),
+                )
+
+        def load_words(g):
+            nc.sync.dma_start(out=word_table[g][:], in_=x_words[g].rearrange("p n t -> p (n t)").bitcast(I32))
+
+        def load_vector(name, vec):
+            tile = keep.tile([P, 8], F32, name=name)
+            runs = vec.rearrange("(m x) o -> m (x o)", x=8)
+            for e in range(2):
+                nc.sync.dma_start(out=tile[e:P:2, 0:7], in_=runs[:, e : e + 7])
+            return tile
+
+        nc.vector.memset(scale_table[:].bitcast(I32), 0)
+        nc.sync.dma_start(offs_t[:], offs)
+        load_weight("w2", w2, 0)
+        load_scales(0)
+        load_words(0)
+        load_scales(1)
+        load_words(1)
+        load_weight("w2", w2, 1)
+        load_weight("w3", w3, 0)
+        nc.sync.dma_start(oth_t[:], oth)
+        lam_t = load_vector("lam_t", lam)
+        unit_t = load_vector("unit_t", unit)
+        load_weight("w3", w3, 1)
+        load_weight("w1", w1, 0)
+        load_weight("w1", w1, 1)
+        raw4 = keep.tile([P, TILES, N], F32, name="raw4", align_bytes=64)
+        w4_rows = w4.rearrange("(m t e) n -> e m t n", t=TILES, e=2)
+        for e in range(2):
+            nc.sync.dma_start(out=raw4[e:P:2, :, :], in_=w4_rows[e])
+
+        grouped, stationary = {}, {}
+
+        def round_weight(engine, name, g, t0, count):
+            tile = keep.tile([P, count * K_PASS], BF16, name=f"bf_{name}{g}_{t0}", tag=f"bf_{name}{g}_{t0}", align_bytes=64)
+            grouped[name, g, t0] = (tile, count)
+            src = raw[name, g][:].rearrange("p j (m t e) -> p m t j e", t=TILES, e=2)[:, :, t0 : t0 + count, :, :]
+            dst = tile[:].rearrange("p (t m e j) -> p m t j e", t=count, e=2, j=PACK)
+            if engine == "vector":
+                nc.vector.tensor_copy(out=dst, in_=src)
+            else:
+                nc.scalar.copy(out=dst, in_=src)
+
+        def quantize(tile, name):
+            width = tile.shape[1] // PACK
+            codes = keep.tile([P, width], U32, name=f"codes_{name}", align_bytes=64)
+            scales = keep.tile([P, width], U8, name=f"scales_{name}", align_bytes=64)
+            nc.vector.quantize_mx(out=codes[:].bitcast(FP8X4), scales=scales[:], in_=tile[:])
+            return codes, scales
+
+        def quantize_weight(name, g, t0):
+            tile, count = grouped[name, g, t0]
+            codes, scales = quantize(tile, f"{name}{g}_{t0}")
+            for i in range(count):
+                cols = slice(i * P, (i + 1) * P)
+                stationary[name, g, t0 + i] = (codes[:, cols], scales[:, cols])
+
+        x_codes = [keep.tile([P, S], U32, name=f"x_codes{g}", align_bytes=64) for g in range(PASSES)]
+        x_planes = keep.tile([P, S], U8, name="x_planes", align_bytes=64)
+
+        def product_pass(acc, name, g, t):
+            codes, scales = stationary[name, g, t]
+            nc.tensor.matmul_mx(
+                out=acc[:],
+                lhsT=codes.bitcast(FP8X4),
+                lhsT_scale=scales,
+                rhs=x_codes[g][:].bitcast(FP8X4),
+                rhs_scale=x_planes[4 * g : P, :],
+                start=(g == 0),
+                stop=(g == PASSES - 1),
+            )
+
+        def prepare(name, g, second_engine):
+            round_weight("vector", name, g, 0, 2)
+            round_weight(second_engine, name, g, 2, 2)
+            quantize_weight(name, g, 0)
+            quantize_weight(name, g, 2)
+
+        def prepare_by_tile(name, g, acc, second_engine):
+            if second_engine == "scalar":
+                for t in range(TILES):
+                    round_weight("vector" if t < 2 else "scalar", name, g, t, 1)
+            else:
+                round_weight("vector", name, g, 0, 1)
+            for t in range(TILES):
+                if second_engine == "vector" and t + 1 < TILES:
+                    round_weight("vector", name, g, t + 1, 1)
+                quantize_weight(name, g, t)
+                product_pass(acc[t], name, g, t)
+
+        prepare("w2", 0, "scalar")
+        nc.vector.tensor_copy(x_codes[0][:], word_table[0][:].bitcast(U32).indirect(offs_t[:]))
+        nc.vector.tensor_copy(x_planes[:], scale_table[:].indirect(offs_t[:]))
+        nc.vector.tensor_copy(x_codes[1][:], word_table[1][:].bitcast(U32).indirect(offs_t[:]))
+        rg = [bank(t) for t in range(TILES)]
+        for t in range(TILES):
+            product_pass(rg[t], "w2", 0, t)
+        prepare_by_tile("w2", 1, rg, "scalar")
+        th = [keep.tile([P, S], F32, name=f"th{t}") for t in range(TILES)]
+        eg = [keep.tile([P, S], F32, name=f"eg{t}") for t in range(TILES)]
+        sums = keep.tile([P, TILES], F32, name="sums")
+        for t in range(TILES):
+            nc.scalar.activation(out=th[t][:], in_=rg[t][:], func=ACT.Tanh)
+        for t in range(TILES):
+            nc.scalar.activation(out=eg[t][:], in_=th[t][:], func=ACT.Exp, scale=2.4, accum_out=sums[:, t : t + 1])
+
+        denom = keep.tile([P, TILES], F32, name="denom")
+        nc.scalar.activation(out=denom[:], in_=sums[:], func=ACT.Copy, scale=1.0 / S, bias=0.2)
+        lam_unit = keep.tile([P, TILES], F32, name="lam_unit")
+        nc.gpsimd.tensor_tensor(lam_unit[:], lam_t[:, 0:7:2], unit_t[:, 0:7:2], ALU.mult)
+
+        rv = [bank(TILES + t) for t in range(TILES)]
+        prepare_by_tile("w3", 0, rv, "vector")
+        prepare_by_tile("w3", 1, rv, "vector")
+        penalty = [keep.tile([P, S], F32, name=f"penalty{t}") for t in range(TILES)]
+        for t in range(TILES):
+            nc.scalar.activation(out=penalty[t][:], in_=rv[t][:], func=ACT.Copy, scale=lam_unit[:, t : t + 1])
+
+        ro = [bank(t) for t in range(TILES)]
+        prepare_by_tile("w1", 0, ro, "vector")
+
+        factor = keep.tile([P, TILES], F32, name="factor", tag="bf_w10_1", align_bytes=64)
+        nc.vector.reciprocal(factor[:], denom[:])
+
+        prepare_by_tile("w1", 1, ro, "scalar")
+        grouped4 = keep.tile([P, N * PACK], BF16, name="grouped4", align_bytes=64)
+        nc.scalar.copy(
+            out=grouped4[:].rearrange("p (c i t) -> p c t i", i=2, t=TILES),
+            in_=raw4[:].rearrange("p t (c i) -> p c t i", i=2),
+        )
+
+        score = keep.tile([P, TILES, S], F32, name="score", align_bytes=64)
+        other = [keep.tile([P, TILES, HALF], F32, name=f"other{h}", align_bytes=64) for h in range(2)]
+
+        def fetch(t, first, count):
+            h, at = divmod(first, HALF)
+            offsets = oth_t[:, first // LIST_ROWS : (first + count) // LIST_ROWS]
+            nc.scalar.activation(out=other[h][:, t, at : at + count], in_=score[:, t, :].indirect(offsets), func=ACT.Copy)
+
+        def score_tile(t):
+            adj = keep.tile([P, S], F32, name=f"adj{t}")
+            halves = [slice(h * HALF, (h + 1) * HALF) for h in range(2)]
+            for cols in halves:
+                nc.vector.scalar_tensor_tensor(
+                    adj[:, cols], ro[t][:, cols], unit_t[:, 2 * t : 2 * t + 1], penalty[t][:, cols], ALU.mult, ALU.subtract
+                )
+            for cols in halves:
+                nc.vector.scalar_tensor_tensor(
+                    score[:, t, cols], adj[:, cols], factor[:, t : t + 1], eg[t][:, cols], ALU.mult, ALU.mult
+                )
+
+        for t in range(TILES):
+            score_tile(t)
+            step = HALF if t < TILES - 1 else PIECE
+            for first in range(0, S, step):
+                fetch(t, first, step)
+        codes4, scales4 = quantize(grouped4, "w4")
+
+        hidden = []
+        for c in range(PIECES):
+            tile = keep.tile([P, PIECE * PACK], BF16, name=f"hidden{c}", align_bytes=64)
+            hidden.append(tile)
+        result = [keep.tile([P, PIECE], F32, name=f"result{c}") for c in range(PIECES)]
+
+        def difference(c):
+            h, at = divmod(c * PIECE, HALF)
+            nc.vector.tensor_tensor(
+                hidden[c][:].rearrange("p (c i t) -> p c t i", i=2, t=TILES),
+                score[:, :, c * PIECE : (c + 1) * PIECE].rearrange("p t (c i) -> p c t i", i=2),
+                other[h][:, :, at : at + PIECE].rearrange("p t (c i) -> p c t i", i=2),
+                ALU.subtract,
+            )
+
+        def finish(c):
+            codes, scales = quantize(hidden[c], f"hidden{c}")
+            acc = bank(TILES + c, PIECE)
+            nc.tensor.matmul_mx(
+                out=acc[:],
+                lhsT=codes4[:].bitcast(FP8X4),
+                lhsT_scale=scales4[:],
+                rhs=codes[:].bitcast(FP8X4),
+                rhs_scale=scales[:],
+                start=True,
+                stop=True,
+            )
+            nc.scalar.copy(out=result[c][:], in_=acc[:])
+            nc.sync.dma_start(out=out[:, c * PIECE : (c + 1) * PIECE], in_=result[c][:])
+
+        for c in range(PIECES + 1):
+            if c < PIECES:
+                difference(c)
+            if c > 0:
+                finish(c - 1)

@@ -48,12 +48,11 @@ def tile_picked_yarmor_pair_p_kernel(
             rows = w[g * K_PASS : (g + 1) * K_PASS, :]
             nc.sync.dma_start(out=raw[name, g][:], in_=rows.rearrange("(p j) c -> p j c", j=PACK))
 
-        def load_scales(g):
+        def load_scales():
             for q in range(4):
-                first = 32 * q + 4 * g
-                nc.sync.dma_start(
-                    out=scale_table[first : first + 4, :].bitcast(I32),
-                    in_=x_scales[g, 4 * q : 4 * q + 4, :].bitcast(I32),
+                nc.gpsimd.dma_start(
+                    out=scale_table[32 * q : 32 * q + 4 * PASSES, :].bitcast(I32),
+                    in_=x_scales[:, 4 * q : 4 * q + 4, :].bitcast(I32),
                 )
 
         def load_words(g):
@@ -63,21 +62,20 @@ def tile_picked_yarmor_pair_p_kernel(
             tile = keep.tile([P, 8], F32, name=name)
             runs = vec.rearrange("(m x) o -> m (x o)", x=8)
             for e in range(2):
-                nc.sync.dma_start(out=tile[e:P:2, 0:7], in_=runs[:, e : e + 7])
+                nc.scalar.dma_start(out=tile[e:P:2, 0:7], in_=runs[:, e : e + 7])
             return tile
 
         nc.vector.memset(scale_table[:].bitcast(I32), 0)
-        nc.sync.dma_start(offs_t[:], offs)
         load_weight("w2", w2, 0)
-        load_scales(0)
+        nc.sync.dma_start(offs_t[:], offs)
+        load_scales()
+        lam_t = load_vector("lam_t", lam)
+        unit_t = load_vector("unit_t", unit)
         load_words(0)
-        load_scales(1)
         load_words(1)
         load_weight("w2", w2, 1)
         load_weight("w3", w3, 0)
         nc.sync.dma_start(oth_t[:], oth)
-        lam_t = load_vector("lam_t", lam)
-        unit_t = load_vector("unit_t", unit)
         load_weight("w3", w3, 1)
         load_weight("w1", w1, 0)
         load_weight("w1", w1, 1)

@@ -44,16 +44,17 @@ def tile_picked_yarmor_pair_p_kernel(
         raw = {}
 
         def load_weight(name, w, g):
-            raw[name, g] = keep.tile([P, PACK, H], F32, name=f"raw_{name}{g}", align_bytes=64)
+            raw[name, g] = keep.tile([P, PACK, H], F32, name=f"raw_{name}{g}", tag=f"raw_{name}{g}", align_bytes=64)
             rows = w[g * K_PASS : (g + 1) * K_PASS, :]
             nc.sync.dma_start(out=raw[name, g][:], in_=rows.rearrange("(p j) c -> p j c", j=PACK))
 
-        def load_scales():
-            for q in range(4):
-                nc.gpsimd.dma_start(
-                    out=scale_table[32 * q : 32 * q + 4 * PASSES, :].bitcast(I32),
-                    in_=x_scales[:, 4 * q : 4 * q + 4, :].bitcast(I32),
-                )
+        def load_scales(rows):
+            for r in rows:
+                for g in range(PASSES):
+                    nc.sync.dma_start(
+                        out=scale_table[4 * g + r : P : 32, :].bitcast(I32),
+                        in_=x_scales[g, r:16:4, :].bitcast(I32),
+                    )
 
         def load_words(g):
             nc.sync.dma_start(out=word_table[g][:], in_=x_words[g].rearrange("p n t -> p (n t)").bitcast(I32))
@@ -62,23 +63,24 @@ def tile_picked_yarmor_pair_p_kernel(
             tile = keep.tile([P, 8], F32, name=name)
             runs = vec.rearrange("(m x) o -> m (x o)", x=8)
             for e in range(2):
-                nc.scalar.dma_start(out=tile[e:P:2, 0:7], in_=runs[:, e : e + 7])
+                nc.sync.dma_start(out=tile[e:P:2, 0:7], in_=runs[:, e : e + 7])
             return tile
 
         nc.vector.memset(scale_table[:].bitcast(I32), 0)
-        load_weight("w2", w2, 0)
         nc.sync.dma_start(offs_t[:], offs)
-        load_scales()
-        lam_t = load_vector("lam_t", lam)
-        unit_t = load_vector("unit_t", unit)
+        load_weight("w2", w2, 0)
+        load_scales((0, 1))
         load_words(0)
+        load_scales((2, 3))
         load_words(1)
         load_weight("w2", w2, 1)
-        load_weight("w3", w3, 0)
-        nc.sync.dma_start(oth_t[:], oth)
-        load_weight("w3", w3, 1)
         load_weight("w1", w1, 0)
+        lam_t = load_vector("lam_t", lam)
+        unit_t = load_vector("unit_t", unit)
         load_weight("w1", w1, 1)
+        load_weight("w3", w3, 0)
+        load_weight("w3", w3, 1)
+        nc.sync.dma_start(oth_t[:], oth)
         raw4 = keep.tile([P, TILES, N], F32, name="raw4", align_bytes=64)
         w4_rows = w4.rearrange("(m t e) n -> e m t n", t=TILES, e=2)
         for e in range(2):
@@ -161,24 +163,22 @@ def tile_picked_yarmor_pair_p_kernel(
 
         denom = keep.tile([P, TILES], F32, name="denom")
         nc.scalar.activation(out=denom[:], in_=sums[:], func=ACT.Copy, scale=1.0 / S, bias=0.2)
-        lam_unit = keep.tile([P, TILES], F32, name="lam_unit")
-        nc.gpsimd.tensor_tensor(lam_unit[:], lam_t[:, 0:7:2], unit_t[:, 0:7:2], ALU.mult)
 
-        rv = [bank(TILES + t) for t in range(TILES)]
-        prepare_by_tile("w3", 0, rv, "vector")
-        prepare_by_tile("w3", 1, rv, "vector")
-        penalty = [keep.tile([P, S], F32, name=f"penalty{t}") for t in range(TILES)]
-        for t in range(TILES):
-            nc.scalar.activation(out=penalty[t][:], in_=rv[t][:], func=ACT.Copy, scale=lam_unit[:, t : t + 1])
-
-        ro = [bank(t) for t in range(TILES)]
+        ro = [bank(TILES + t) for t in range(TILES)]
         prepare_by_tile("w1", 0, ro, "vector")
+        prepare_by_tile("w1", 1, ro, "vector")
+        objective = [keep.tile([P, S], F32, name=f"objective{t}") for t in range(TILES)]
+        for t in range(TILES):
+            nc.scalar.copy(out=objective[t][:], in_=ro[t][:])
 
-        factor = keep.tile([P, TILES], F32, name="factor", tag="bf_w10_1", align_bytes=64)
-        nc.vector.reciprocal(factor[:], denom[:])
-
-        prepare_by_tile("w1", 1, ro, "scalar")
-        grouped4 = keep.tile([P, N * PACK], BF16, name="grouped4", align_bytes=64)
+        rv = [bank(t) for t in range(TILES)]
+        prepare_by_tile("w3", 0, rv, "vector")
+        recip = keep.tile([P, TILES], F32, name="recip", tag="bf_w30_1", align_bytes=64)
+        nc.vector.reciprocal(recip[:], denom[:])
+        factor = keep.tile([P, TILES], F32, name="factor", tag="bf_w30_2", align_bytes=64)
+        nc.vector.tensor_tensor(factor[:], recip[:], unit_t[:, 0:7:2], ALU.mult)
+        prepare_by_tile("w3", 1, rv, "scalar")
+        grouped4 = keep.tile([P, N * PACK], BF16, name="grouped4", tag="raw_w31", align_bytes=64)
         nc.scalar.copy(
             out=grouped4[:].rearrange("p (c i t) -> p c t i", i=2, t=TILES),
             in_=raw4[:].rearrange("p t (c i) -> p c t i", i=2),
@@ -197,7 +197,7 @@ def tile_picked_yarmor_pair_p_kernel(
             halves = [slice(h * HALF, (h + 1) * HALF) for h in range(2)]
             for cols in halves:
                 nc.vector.scalar_tensor_tensor(
-                    adj[:, cols], ro[t][:, cols], unit_t[:, 2 * t : 2 * t + 1], penalty[t][:, cols], ALU.mult, ALU.subtract
+                    adj[:, cols], rv[t][:, cols], lam_t[:, 2 * t : 2 * t + 1], objective[t][:, cols], ALU.mult, ALU.subtract
                 )
             for cols in halves:
                 nc.vector.scalar_tensor_tensor(
@@ -221,8 +221,8 @@ def tile_picked_yarmor_pair_p_kernel(
             h, at = divmod(c * PIECE, HALF)
             nc.vector.tensor_tensor(
                 hidden[c][:].rearrange("p (c i t) -> p c t i", i=2, t=TILES),
-                score[:, :, c * PIECE : (c + 1) * PIECE].rearrange("p t (c i) -> p c t i", i=2),
                 other[h][:, :, at : at + PIECE].rearrange("p t (c i) -> p c t i", i=2),
+                score[:, :, c * PIECE : (c + 1) * PIECE].rearrange("p t (c i) -> p c t i", i=2),
                 ALU.subtract,
             )
 

@@ -21,9 +21,9 @@ K_PASS = P * PACK
 PASSES = K // K_PASS
 TILES = H // P
 HALF = S // 2
-PIECE = 128
-PIECES = S // PIECE
+PIECES = ((0, 128), (128, 128), (256, 128), (384, 64), (448, 64))
 LIST_ROWS = 16
+BANKS = 8
 
 
 def tile_picked_yarmor_pair_p_kernel(
@@ -67,8 +67,8 @@ def tile_picked_yarmor_pair_p_kernel(
             return tile
 
         nc.vector.memset(scale_table[:].bitcast(I32), 0)
-        nc.sync.dma_start(offs_t[:], offs)
         load_weight("w2", w2, 0)
+        nc.sync.dma_start(offs_t[:], offs)
         load_scales((0, 1))
         load_words(0)
         load_scales((2, 3))
@@ -187,10 +187,14 @@ def tile_picked_yarmor_pair_p_kernel(
         score = keep.tile([P, TILES, S], F32, name="score", align_bytes=64)
         other = [keep.tile([P, TILES, HALF], F32, name=f"other{h}", align_bytes=64) for h in range(2)]
 
-        def fetch(t, first, count):
+        def fetch(engine, t, first, count):
             h, at = divmod(first, HALF)
             offsets = oth_t[:, first // LIST_ROWS : (first + count) // LIST_ROWS]
-            nc.scalar.activation(out=other[h][:, t, at : at + count], in_=score[:, t, :].indirect(offsets), func=ACT.Copy)
+            window = score[:, t, :].indirect(offsets)
+            if engine == "vector":
+                nc.vector.tensor_copy(other[h][:, t, at : at + count], window)
+            else:
+                nc.scalar.activation(out=other[h][:, t, at : at + count], in_=window, func=ACT.Copy)
 
         def score_tile(t):
             adj = keep.tile([P, S], F32, name=f"adj{t}")
@@ -206,29 +210,28 @@ def tile_picked_yarmor_pair_p_kernel(
 
         for t in range(TILES):
             score_tile(t)
-            step = HALF if t < TILES - 1 else PIECE
-            for first in range(0, S, step):
-                fetch(t, first, step)
+            if t < TILES - 1:
+                fetch("scalar", t, 0, HALF)
+                fetch("scalar", t, HALF, HALF)
         codes4, scales4 = quantize(grouped4, "w4")
+        for first, count in PIECES:
+            fetch("vector" if first < HALF else "scalar", TILES - 1, first, count)
 
-        hidden = []
-        for c in range(PIECES):
-            tile = keep.tile([P, PIECE * PACK], BF16, name=f"hidden{c}", align_bytes=64)
-            hidden.append(tile)
-        result = [keep.tile([P, PIECE], F32, name=f"result{c}") for c in range(PIECES)]
+        hidden = {}
 
-        def difference(c):
-            h, at = divmod(c * PIECE, HALF)
+        def difference(first, count):
+            h, at = divmod(first, HALF)
+            hidden[first] = keep.tile([P, count * PACK], BF16, name=f"hidden{first}", align_bytes=64)
             nc.vector.tensor_tensor(
-                hidden[c][:].rearrange("p (c i t) -> p c t i", i=2, t=TILES),
-                other[h][:, :, at : at + PIECE].rearrange("p t (c i) -> p c t i", i=2),
-                score[:, :, c * PIECE : (c + 1) * PIECE].rearrange("p t (c i) -> p c t i", i=2),
+                hidden[first][:].rearrange("p (c i t) -> p c t i", i=2, t=TILES),
+                other[h][:, :, at : at + count].rearrange("p t (c i) -> p c t i", i=2),
+                score[:, :, first : first + count].rearrange("p t (c i) -> p c t i", i=2),
                 ALU.subtract,
             )
 
-        def finish(c):
-            codes, scales = quantize(hidden[c], f"hidden{c}")
-            acc = bank(TILES + c, PIECE)
+        def finish(c, first, count):
+            codes, scales = quantize(hidden[first], f"hidden{first}")
+            acc = bank((TILES + c) % BANKS, count)
             nc.tensor.matmul_mx(
                 out=acc[:],
                 lhsT=codes4[:].bitcast(FP8X4),
@@ -238,11 +241,12 @@ def tile_picked_yarmor_pair_p_kernel(
                 start=True,
                 stop=True,
             )
-            nc.scalar.copy(out=result[c][:], in_=acc[:])
-            nc.sync.dma_start(out=out[:, c * PIECE : (c + 1) * PIECE], in_=result[c][:])
+            result = keep.tile([P, count], F32, name=f"result{first}")
+            nc.scalar.copy(out=result[:], in_=acc[:])
+            nc.sync.dma_start(out=out[:, first : first + count], in_=result[:])
 
-        for c in range(PIECES + 1):
-            if c < PIECES:
-                difference(c)
+        for c in range(len(PIECES) + 1):
+            if c < len(PIECES):
+                difference(*PIECES[c])
             if c > 0:
-                finish(c - 1)
+                finish(c - 1, *PIECES[c - 1])

@@ -20,10 +20,15 @@ PACK = 4
 K_PASS = P * PACK
 PASSES = K // K_PASS
 TILES = H // P
-HALF = S // 2
-PIECES = ((0, 128), (128, 128), (256, 128), (384, 64), (448, 64))
+PAIR = 2
+RUN = PAIR * TILES
+QUADRANT = 32
+SCALE_ROWS = 4
 LIST_ROWS = 16
 BANKS = 8
+HALF = S // 2
+VECTOR_TILES = 2
+PIECES = ((0, 128), (128, 128), (256, 128), (384, 64), (448, 64))
 
 
 def tile_picked_yarmor_pair_p_kernel(
@@ -48,22 +53,22 @@ def tile_picked_yarmor_pair_p_kernel(
             rows = w[g * K_PASS : (g + 1) * K_PASS, :]
             nc.sync.dma_start(out=raw[name, g][:], in_=rows.rearrange("(p j) c -> p j c", j=PACK))
 
-        def load_scales(rows):
-            for r in rows:
+        def load_scales(scale_rows):
+            for r in scale_rows:
                 for g in range(PASSES):
                     nc.sync.dma_start(
-                        out=scale_table[4 * g + r : P : 32, :].bitcast(I32),
-                        in_=x_scales[g, r:16:4, :].bitcast(I32),
+                        out=scale_table[SCALE_ROWS * g + r : P : QUADRANT, :].bitcast(I32),
+                        in_=x_scales[g, r : K_PASS // QUADRANT : SCALE_ROWS, :].bitcast(I32),
                     )
 
         def load_words(g):
             nc.sync.dma_start(out=word_table[g][:], in_=x_words[g].rearrange("p n t -> p (n t)").bitcast(I32))
 
         def load_vector(name, vec):
-            tile = keep.tile([P, 8], F32, name=name)
-            runs = vec.rearrange("(m x) o -> m (x o)", x=8)
-            for e in range(2):
-                nc.sync.dma_start(out=tile[e:P:2, 0:7], in_=runs[:, e : e + 7])
+            tile = keep.tile([P, RUN], F32, name=name)
+            runs = vec.rearrange("(m x) o -> m (x o)", x=RUN)
+            for e in range(PAIR):
+                nc.sync.dma_start(out=tile[e:P:PAIR, 0 : RUN - 1], in_=runs[:, e : e + RUN - 1])
             return tile
 
         nc.vector.memset(scale_table[:].bitcast(I32), 0)
@@ -75,24 +80,25 @@ def tile_picked_yarmor_pair_p_kernel(
         load_words(1)
         load_weight("w2", w2, 1)
         load_weight("w1", w1, 0)
-        lam_t = load_vector("lam_t", lam)
-        unit_t = load_vector("unit_t", unit)
         load_weight("w1", w1, 1)
         load_weight("w3", w3, 0)
         load_weight("w3", w3, 1)
+        unit_t = load_vector("unit_t", unit)
+        lam_t = load_vector("lam_t", lam)
         nc.sync.dma_start(oth_t[:], oth)
         raw4 = keep.tile([P, TILES, N], F32, name="raw4", align_bytes=64)
-        w4_rows = w4.rearrange("(m t e) n -> e m t n", t=TILES, e=2)
-        for e in range(2):
-            nc.sync.dma_start(out=raw4[e:P:2, :, :], in_=w4_rows[e])
+        w4_rows = w4.rearrange("(m t e) n -> e m t n", t=TILES, e=PAIR)
+        for e in range(PAIR):
+            nc.sync.dma_start(out=raw4[e:P:PAIR, :, :], in_=w4_rows[e])
 
         grouped, stationary = {}, {}
 
         def round_weight(engine, name, g, t0, count):
-            tile = keep.tile([P, count * K_PASS], BF16, name=f"bf_{name}{g}_{t0}", tag=f"bf_{name}{g}_{t0}", align_bytes=64)
+            label = f"bf_{name}{g}_{t0}"
+            tile = keep.tile([P, count * K_PASS], BF16, name=label, tag=label, align_bytes=64)
             grouped[name, g, t0] = (tile, count)
-            src = raw[name, g][:].rearrange("p j (m t e) -> p m t j e", t=TILES, e=2)[:, :, t0 : t0 + count, :, :]
-            dst = tile[:].rearrange("p (t m e j) -> p m t j e", t=count, e=2, j=PACK)
+            src = raw[name, g][:].rearrange("p j (m t e) -> p m t j e", t=TILES, e=PAIR)[:, :, t0 : t0 + count, :, :]
+            dst = tile[:].rearrange("p (t m e j) -> p m t j e", t=count, e=PAIR, j=PACK)
             if engine == "vector":
                 nc.vector.tensor_copy(out=dst, in_=src)
             else:
@@ -122,37 +128,37 @@ def tile_picked_yarmor_pair_p_kernel(
                 lhsT=codes.bitcast(FP8X4),
                 lhsT_scale=scales,
                 rhs=x_codes[g][:].bitcast(FP8X4),
-                rhs_scale=x_planes[4 * g : P, :],
+                rhs_scale=x_planes[SCALE_ROWS * g : P, :],
                 start=(g == 0),
                 stop=(g == PASSES - 1),
             )
 
-        def prepare(name, g, second_engine):
-            round_weight("vector", name, g, 0, 2)
-            round_weight(second_engine, name, g, 2, 2)
-            quantize_weight(name, g, 0)
-            quantize_weight(name, g, 2)
-
-        def prepare_by_tile(name, g, acc, second_engine):
-            if second_engine == "scalar":
-                for t in range(TILES):
-                    round_weight("vector" if t < 2 else "scalar", name, g, t, 1)
-            else:
-                round_weight("vector", name, g, 0, 1)
+        def pass_on_two_engines(name, g, acc):
             for t in range(TILES):
-                if second_engine == "vector" and t + 1 < TILES:
+                round_weight("vector" if t < VECTOR_TILES else "scalar", name, g, t, 1)
+            for t in range(TILES):
+                quantize_weight(name, g, t)
+                product_pass(acc[t], name, g, t)
+
+        def pass_on_vector(name, g, acc):
+            round_weight("vector", name, g, 0, 1)
+            for t in range(TILES):
+                if t + 1 < TILES:
                     round_weight("vector", name, g, t + 1, 1)
                 quantize_weight(name, g, t)
                 product_pass(acc[t], name, g, t)
 
-        prepare("w2", 0, "scalar")
+        round_weight("vector", "w2", 0, 0, VECTOR_TILES)
+        round_weight("scalar", "w2", 0, VECTOR_TILES, TILES - VECTOR_TILES)
+        quantize_weight("w2", 0, 0)
+        quantize_weight("w2", 0, VECTOR_TILES)
         nc.vector.tensor_copy(x_codes[0][:], word_table[0][:].bitcast(U32).indirect(offs_t[:]))
         nc.vector.tensor_copy(x_planes[:], scale_table[:].indirect(offs_t[:]))
         nc.vector.tensor_copy(x_codes[1][:], word_table[1][:].bitcast(U32).indirect(offs_t[:]))
         rg = [bank(t) for t in range(TILES)]
         for t in range(TILES):
             product_pass(rg[t], "w2", 0, t)
-        prepare_by_tile("w2", 1, rg, "scalar")
+        pass_on_two_engines("w2", 1, rg)
         th = [keep.tile([P, S], F32, name=f"th{t}") for t in range(TILES)]
         eg = [keep.tile([P, S], F32, name=f"eg{t}") for t in range(TILES)]
         sums = keep.tile([P, TILES], F32, name="sums")
@@ -160,48 +166,48 @@ def tile_picked_yarmor_pair_p_kernel(
             nc.scalar.activation(out=th[t][:], in_=rg[t][:], func=ACT.Tanh)
         for t in range(TILES):
             nc.scalar.activation(out=eg[t][:], in_=th[t][:], func=ACT.Exp, scale=2.4, accum_out=sums[:, t : t + 1])
-
         denom = keep.tile([P, TILES], F32, name="denom")
         nc.scalar.activation(out=denom[:], in_=sums[:], func=ACT.Copy, scale=1.0 / S, bias=0.2)
 
         ro = [bank(TILES + t) for t in range(TILES)]
-        prepare_by_tile("w1", 0, ro, "vector")
-        prepare_by_tile("w1", 1, ro, "vector")
+        pass_on_vector("w1", 0, ro)
+        pass_on_vector("w1", 1, ro)
         objective = [keep.tile([P, S], F32, name=f"objective{t}") for t in range(TILES)]
         for t in range(TILES):
             nc.scalar.copy(out=objective[t][:], in_=ro[t][:])
 
         rv = [bank(t) for t in range(TILES)]
-        prepare_by_tile("w3", 0, rv, "vector")
+        pass_on_vector("w3", 0, rv)
         recip = keep.tile([P, TILES], F32, name="recip", tag="bf_w30_1", align_bytes=64)
         nc.vector.reciprocal(recip[:], denom[:])
-        factor = keep.tile([P, TILES], F32, name="factor", tag="bf_w30_2", align_bytes=64)
-        nc.vector.tensor_tensor(factor[:], recip[:], unit_t[:, 0:7:2], ALU.mult)
-        prepare_by_tile("w3", 1, rv, "scalar")
+        pass_on_two_engines("w3", 1, rv)
+        factor = keep.tile([P, TILES], F32, name="factor", tag="bf_w31_0", align_bytes=64)
+        nc.vector.tensor_tensor(factor[:], recip[:], unit_t[:, 0 : RUN - 1 : PAIR], ALU.mult)
         grouped4 = keep.tile([P, N * PACK], BF16, name="grouped4", tag="raw_w31", align_bytes=64)
         nc.scalar.copy(
-            out=grouped4[:].rearrange("p (c i t) -> p c t i", i=2, t=TILES),
-            in_=raw4[:].rearrange("p t (c i) -> p c t i", i=2),
+            out=grouped4[:].rearrange("p (c i t) -> p c t i", i=PAIR, t=TILES),
+            in_=raw4[:].rearrange("p t (c i) -> p c t i", i=PAIR),
         )
 
         score = keep.tile([P, TILES, S], F32, name="score", align_bytes=64)
-        other = [keep.tile([P, TILES, HALF], F32, name=f"other{h}", align_bytes=64) for h in range(2)]
+        other = [keep.tile([P, TILES, HALF], F32, name=f"other{h}", align_bytes=64) for h in range(S // HALF)]
 
         def fetch(engine, t, first, count):
             h, at = divmod(first, HALF)
             offsets = oth_t[:, first // LIST_ROWS : (first + count) // LIST_ROWS]
-            window = score[:, t, :].indirect(offsets)
+            picked = score[:, t, :].indirect(offsets)
             if engine == "vector":
-                nc.vector.tensor_copy(other[h][:, t, at : at + count], window)
+                nc.vector.tensor_copy(other[h][:, t, at : at + count], picked)
             else:
-                nc.scalar.activation(out=other[h][:, t, at : at + count], in_=window, func=ACT.Copy)
+                nc.scalar.activation(out=other[h][:, t, at : at + count], in_=picked, func=ACT.Copy)
 
         def score_tile(t):
             adj = keep.tile([P, S], F32, name=f"adj{t}")
-            halves = [slice(h * HALF, (h + 1) * HALF) for h in range(2)]
+            lam_col = lam_t[:, PAIR * t : PAIR * t + 1]
+            halves = [slice(first, first + HALF) for first in range(0, S, HALF)]
             for cols in halves:
                 nc.vector.scalar_tensor_tensor(
-                    adj[:, cols], rv[t][:, cols], lam_t[:, 2 * t : 2 * t + 1], objective[t][:, cols], ALU.mult, ALU.subtract
+                    adj[:, cols], rv[t][:, cols], lam_col, objective[t][:, cols], ALU.mult, ALU.subtract
                 )
             for cols in halves:
                 nc.vector.scalar_tensor_tensor(
@@ -223,15 +229,15 @@ def tile_picked_yarmor_pair_p_kernel(
             h, at = divmod(first, HALF)
             hidden[first] = keep.tile([P, count * PACK], BF16, name=f"hidden{first}", align_bytes=64)
             nc.vector.tensor_tensor(
-                hidden[first][:].rearrange("p (c i t) -> p c t i", i=2, t=TILES),
-                other[h][:, :, at : at + count].rearrange("p t (c i) -> p c t i", i=2),
-                score[:, :, first : first + count].rearrange("p t (c i) -> p c t i", i=2),
+                hidden[first][:].rearrange("p (c i t) -> p c t i", i=PAIR, t=TILES),
+                other[h][:, :, at : at + count].rearrange("p t (c i) -> p c t i", i=PAIR),
+                score[:, :, first : first + count].rearrange("p t (c i) -> p c t i", i=PAIR),
                 ALU.subtract,
             )
 
-        def finish(c, first, count):
+        def finish(piece, first, count):
             codes, scales = quantize(hidden[first], f"hidden{first}")
-            acc = bank((TILES + c) % BANKS, count)
+            acc = bank((TILES + piece) % BANKS, count)
             nc.tensor.matmul_mx(
                 out=acc[:],
                 lhsT=codes4[:].bitcast(FP8X4),
@@ -245,8 +251,8 @@ def tile_picked_yarmor_pair_p_kernel(
             nc.scalar.copy(out=result[:], in_=acc[:])
             nc.sync.dma_start(out=out[:, first : first + count], in_=result[:])
 
-        for c in range(len(PIECES) + 1):
-            if c < len(PIECES):
-                difference(*PIECES[c])
-            if c > 0:
-                finish(c - 1, *PIECES[c - 1])
+        difference(*PIECES[0])
+        for piece in range(len(PIECES)):
+            if piece + 1 < len(PIECES):
+                difference(*PIECES[piece + 1])
+            finish(piece, *PIECES[piece])

from contextlib import ExitStack

import concourse.mybir as mybir

K, T, S, N, H = 1024, 2048, 512, 128, 512
FLOPS = 2 * (3 * K * H * S + H * N * S)

F32 = mybir.dt.float32
BF16 = mybir.dt.bfloat16
I32 = mybir.dt.int32
U32 = mybir.dt.uint32
U16 = mybir.dt.uint16
U8 = mybir.dt.uint8
FP8X4 = mybir.dt.float8_e4m3fn_x4
ALU = mybir.AluOpType
ACT = mybir.ActivationFunctionType

P = 128
PACK = 4
K_PASS = P * PACK
PASSES = K // K_PASS
TILES = H // P
PAIR = 2
RUN = PAIR * TILES
QUADRANT = 32
SCALE_ROWS = 4
LIST_ROWS = 16
BANKS = 8
HALF = S // 2
VECTOR_TILES = 2
PIECES = ((0, 128), (128, 128), (256, 128), (384, 64), (448, 64))


def tile_picked_yarmor_pair_p_kernel(
    tc, x_words, x_scales, w1, w2, w3, lam, unit, w4, offs, oth, out
):
    nc = tc.nc
    with ExitStack() as ctx:
        keep = ctx.enter_context(tc.tile_pool(name="keep", bufs=1))
        psum = ctx.enter_context(tc.psum_pool(name="psum", bufs=1))

        def bank(b, width=S):
            return psum.tile([P, width], F32, name=f"bank{b}", tag=f"bank{b}")

        offs_t = keep.tile([P, S // LIST_ROWS], U16, name="offs_t")
        oth_t = keep.tile([P, S // LIST_ROWS], U16, name="oth_t")
        scale_table = keep.tile([P, T], U8, name="scale_table", align_bytes=64)
        word_table = [keep.tile([P, T], I32, name=f"word_table{g}", align_bytes=64) for g in range(PASSES)]
        raw = {}

        def load_weight(name, w, g):
            raw[name, g] = keep.tile([P, PACK, H], F32, name=f"raw_{name}{g}", tag=f"raw_{name}{g}", align_bytes=64)
            rows = w[g * K_PASS : (g + 1) * K_PASS, :]
            nc.sync.dma_start(out=raw[name, g][:], in_=rows.rearrange("(p j) c -> p j c", j=PACK))

        def load_scales(scale_rows):
            for r in scale_rows:
                for g in range(PASSES):
                    nc.sync.dma_start(
                        out=scale_table[SCALE_ROWS * g + r : P : QUADRANT, :].bitcast(I32),
                        in_=x_scales[g, r : K_PASS // QUADRANT : SCALE_ROWS, :].bitcast(I32),
                    )

        def load_words(g):
            nc.sync.dma_start(out=word_table[g][:], in_=x_words[g].rearrange("p n t -> p (n t)").bitcast(I32))

        def load_vector(name, vec):
            tile = keep.tile([P, RUN], F32, name=name)
            runs = vec.rearrange("(m x) o -> m (x o)", x=RUN)
            for e in range(PAIR):
                nc.sync.dma_start(out=tile[e:P:PAIR, 0 : RUN - 1], in_=runs[:, e : e + RUN - 1])
            return tile

        nc.vector.memset(scale_table[:].bitcast(I32), 0)
        load_weight("w2", w2, 0)
        nc.sync.dma_start(offs_t[:], offs)
        load_scales((0, 1))
        load_words(0)
        load_scales((2, 3))
        load_words(1)
        load_weight("w2", w2, 1)
        load_weight("w1", w1, 0)
        load_weight("w1", w1, 1)
        load_weight("w3", w3, 0)
        load_weight("w3", w3, 1)
        unit_t = load_vector("unit_t", unit)
        lam_t = load_vector("lam_t", lam)
        nc.sync.dma_start(oth_t[:], oth)
        raw4 = keep.tile([P, TILES, N], F32, name="raw4", align_bytes=64)
        w4_rows = w4.rearrange("(m t e) n -> e m t n", t=TILES, e=PAIR)
        for e in range(PAIR):
            nc.sync.dma_start(out=raw4[e:P:PAIR, :, :], in_=w4_rows[e])

        grouped, stationary = {}, {}

        def round_weight(engine, name, g, t0, count):
            label = f"bf_{name}{g}_{t0}"
            tile = keep.tile([P, count * K_PASS], BF16, name=label, tag=label, align_bytes=64)
            grouped[name, g, t0] = (tile, count)
            src = raw[name, g][:].rearrange("p j (m t e) -> p m t j e", t=TILES, e=PAIR)[:, :, t0 : t0 + count, :, :]
            dst = tile[:].rearrange("p (t m e j) -> p m t j e", t=count, e=PAIR, j=PACK)
            if engine == "vector":
                nc.vector.tensor_copy(out=dst, in_=src)
            else:
                nc.scalar.copy(out=dst, in_=src)

        def quantize(tile, name):
            width = tile.shape[1] // PACK
            codes = keep.tile([P, width], U32, name=f"codes_{name}", align_bytes=64)
            scales = keep.tile([P, width], U8, name=f"scales_{name}", align_bytes=64)
            nc.vector.quantize_mx(out=codes[:].bitcast(FP8X4), scales=scales[:], in_=tile[:])
            return codes, scales

        def quantize_weight(name, g, t0):
            tile, count = grouped[name, g, t0]
            codes, scales = quantize(tile, f"{name}{g}_{t0}")
            for i in range(count):
                cols = slice(i * P, (i + 1) * P)
                stationary[name, g, t0 + i] = (codes[:, cols], scales[:, cols])

        x_codes = [keep.tile([P, S], U32, name=f"x_codes{g}", align_bytes=64) for g in range(PASSES)]
        x_planes = keep.tile([P, S], U8, name="x_planes", align_bytes=64)

        def product_pass(acc, name, g, t):
            codes, scales = stationary[name, g, t]
            nc.tensor.matmul_mx(
                out=acc[:],
                lhsT=codes.bitcast(FP8X4),
                lhsT_scale=scales,
                rhs=x_codes[g][:].bitcast(FP8X4),
                rhs_scale=x_planes[SCALE_ROWS * g : P, :],
                start=(g == 0),
                stop=(g == PASSES - 1),
            )

        def pass_on_two_engines(name, g, acc):
            for t in range(TILES):
                round_weight("vector" if t < VECTOR_TILES else "scalar", name, g, t, 1)
            for t in range(TILES):
                quantize_weight(name, g, t)
                product_pass(acc[t], name, g, t)

        def pass_on_vector(name, g, acc):
            round_weight("vector", name, g, 0, 1)
            for t in range(TILES):
                if t + 1 < TILES:
                    round_weight("vector", name, g, t + 1, 1)
                quantize_weight(name, g, t)
                product_pass(acc[t], name, g, t)

        round_weight("vector", "w2", 0, 0, VECTOR_TILES)
        round_weight("scalar", "w2", 0, VECTOR_TILES, TILES - VECTOR_TILES)
        quantize_weight("w2", 0, 0)
        quantize_weight("w2", 0, VECTOR_TILES)
        nc.vector.tensor_copy(x_codes[0][:], word_table[0][:].bitcast(U32).indirect(offs_t[:]))
        nc.vector.tensor_copy(x_planes[:], scale_table[:].indirect(offs_t[:]))
        nc.vector.tensor_copy(x_codes[1][:], word_table[1][:].bitcast(U32).indirect(offs_t[:]))
        rg = [bank(t) for t in range(TILES)]
        for t in range(TILES):
            product_pass(rg[t], "w2", 0, t)
        pass_on_two_engines("w2", 1, rg)
        th = [keep.tile([P, S], F32, name=f"th{t}") for t in range(TILES)]
        eg = [keep.tile([P, S], F32, name=f"eg{t}") for t in range(TILES)]
        sums = keep.tile([P, TILES], F32, name="sums")
        for t in range(TILES):
            nc.scalar.activation(out=th[t][:], in_=rg[t][:], func=ACT.Tanh)
        for t in range(TILES):
            nc.scalar.activation(out=eg[t][:], in_=th[t][:], func=ACT.Exp, scale=2.4, accum_out=sums[:, t : t + 1])
        denom = keep.tile([P, TILES], F32, name="denom")
        nc.scalar.activation(out=denom[:], in_=sums[:], func=ACT.Copy, scale=1.0 / S, bias=0.2)

        ro = [bank(TILES + t) for t in range(TILES)]
        pass_on_vector("w1", 0, ro)
        pass_on_vector("w1", 1, ro)
        objective = [keep.tile([P, S], F32, name=f"objective{t}") for t in range(TILES)]
        for t in range(TILES):
            nc.scalar.copy(out=objective[t][:], in_=ro[t][:])

        rv = [bank(t) for t in range(TILES)]
        pass_on_vector("w3", 0, rv)
        recip = keep.tile([P, TILES], F32, name="recip", tag="bf_w30_1", align_bytes=64)
        nc.vector.reciprocal(recip[:], denom[:])
        pass_on_two_engines("w3", 1, rv)
        factor = keep.tile([P, TILES], F32, name="factor", tag="bf_w31_0", align_bytes=64)
        nc.vector.tensor_tensor(factor[:], recip[:], unit_t[:, 0 : RUN - 1 : PAIR], ALU.mult)
        grouped4 = keep.tile([P, N * PACK], BF16, name="grouped4", tag="raw_w31", align_bytes=64)
        nc.scalar.copy(
            out=grouped4[:].rearrange("p (c i t) -> p c t i", i=PAIR, t=TILES),
            in_=raw4[:].rearrange("p t (c i) -> p c t i", i=PAIR),
        )

        score = keep.tile([P, TILES, S], F32, name="score", align_bytes=64)
        other = [keep.tile([P, TILES, HALF], F32, name=f"other{h}", align_bytes=64) for h in range(S // HALF)]

        def fetch(engine, t, first, count):
            h, at = divmod(first, HALF)
            offsets = oth_t[:, first // LIST_ROWS : (first + count) // LIST_ROWS]
            picked = score[:, t, :].indirect(offsets)
            if engine == "vector":
                nc.vector.tensor_copy(other[h][:, t, at : at + count], picked)
            else:
                nc.scalar.activation(out=other[h][:, t, at : at + count], in_=picked, func=ACT.Copy)

        def score_tile(t):
            adj = keep.tile([P, S], F32, name=f"adj{t}")
            lam_col = lam_t[:, PAIR * t : PAIR * t + 1]
            halves = [slice(first, first + HALF) for first in range(0, S, HALF)]
            for cols in halves:
                nc.vector.scalar_tensor_tensor(
                    adj[:, cols], rv[t][:, cols], lam_col, objective[t][:, cols], ALU.mult, ALU.subtract
                )
            for cols in halves:
                nc.vector.scalar_tensor_tensor(
                    score[:, t, cols], adj[:, cols], factor[:, t : t + 1], eg[t][:, cols], ALU.mult, ALU.mult
                )

        for t in range(TILES):
            score_tile(t)
            if t < TILES - 1:
                fetch("scalar", t, 0, HALF)
                fetch("scalar", t, HALF, HALF)
        codes4, scales4 = quantize(grouped4, "w4")
        for first, count in PIECES:
            fetch("vector" if first < HALF else "scalar", TILES - 1, first, count)

        hidden = {}

        def difference(first, count):
            h, at = divmod(first, HALF)
            hidden[first] = keep.tile([P, count * PACK], BF16, name=f"hidden{first}", align_bytes=64)
            nc.vector.tensor_tensor(
                hidden[first][:].rearrange("p (c i t) -> p c t i", i=PAIR, t=TILES),
                other[h][:, :, at : at + count].rearrange("p t (c i) -> p c t i", i=PAIR),
                score[:, :, first : first + count].rearrange("p t (c i) -> p c t i", i=PAIR),
                ALU.subtract,
            )

        def finish(piece, first, count):
            codes, scales = quantize(hidden[first], f"hidden{first}")
            acc = bank((TILES + piece) % BANKS, count)
            nc.tensor.matmul_mx(
                out=acc[:],
                lhsT=codes4[:].bitcast(FP8X4),
                lhsT_scale=scales4[:],
                rhs=codes[:].bitcast(FP8X4),
                rhs_scale=scales[:],
                start=True,
                stop=True,
            )
            result = keep.tile([P, count], F32, name=f"result{first}")
            nc.scalar.copy(out=result[:], in_=acc[:])
            nc.sync.dma_start(out=out[:, first : first + count], in_=result[:])

        difference(*PIECES[0])
        for piece in range(len(PIECES)):
            if piece + 1 < len(PIECES):
                difference(*PIECES[piece + 1])
            finish(piece, *PIECES[piece])
